import numpy as np
import ml_dtypes


def mxq(x, axis, fmt="e4m3"):
    dtype, down = {"e4m3": (ml_dtypes.float8_e4m3fn, 7), "e5m2": (ml_dtypes.float8_e5m2, 14)}[fmt]
    v = np.moveaxis(np.asarray(x, np.float32).astype(ml_dtypes.bfloat16).astype(np.float64), axis, -1)
    blocks = v.reshape(v.shape[:-1] + (-1, 32))
    amax = np.abs(blocks).max(-1, keepdims=True)
    byte = np.maximum(np.where(amax > 0, np.frexp(amax)[1] - 1 + 127, 0) - down, 1)
    scale = np.exp2(byte - 127.0)
    codes = (blocks / scale).astype(np.float32).astype(dtype).astype(np.float64)
    return np.moveaxis((codes * scale).reshape(v.shape), -1, axis)


WIDE = False


def mx_kscale(k, group=512):
    if not WIDE:
        return np.ones(k)
    levels = np.array([10, -10, 5, -5, 0])
    if group != 512:
        return np.exp2(np.random.permutation(np.resize(levels, k // group))).repeat(group)
    if k % 512:
        return np.exp2(np.random.permutation(np.resize(levels, k // 32))).repeat(32)
    a = np.empty((k // 512, 16))
    for p in range(k // 512):
        a[p, :8] = np.random.permutation(np.resize(levels, 8))
        for g in range(8):
            far = levels[np.abs(levels - a[p, g]) >= 10]
            a[p, g + 8] = far[np.random.randint(len(far))]
    return np.exp2(a.ravel()).repeat(32)


def f64(x):
    return np.asarray(x).astype(np.float64)


G, D, M, N = 4, 256, 128, 512


def setup_inputs():
    n = np.random.standard_normal
    s = mx_kscale(D, 0)[:, None]
    return {
        "x": (n((G, D, N)) * s).astype(np.float32),
        "w": (n((G, D, M)) / np.sqrt(D) / s).astype(np.float32),
        "b": (0.5 * n((G, M, 1))).astype(np.float32),
    }


def reference(x, w, b):
    xq = mxq(f64(x), 1, "e4m3")
    y = mxq(f64(w), 1, "e4m3").transpose(0, 2, 1) @ xq
    y = y + f64(b)
    y = np.square(np.maximum(y, 0.0))
    return y

@@ -1,0 +1,187 @@
+from contextlib import ExitStack
+
+import concourse.mybir as mybir
+
+G, D, M, N = 4, 256, 128, 512
+FLOPS = 2 * G * D * M * N
+
+F32 = mybir.dt.float32
+BF16 = mybir.dt.bfloat16
+U32 = mybir.dt.uint32
+U8 = mybir.dt.uint8
+FP8X4 = mybir.dt.float8_e4m3fn_x4
+ALU = mybir.AluOpType
+ACT = mybir.ActivationFunctionType
+
+P = 128
+PACK = 4
+ROWS = D // PACK
+N_MM = 128
+QUAD = 32
+
+
+def tile_rows_glin_relu2_bias_kernel(tc, x, w, b, out):
+    nc = tc.nc
+    x_pairs = x.rearrange("(a c) (p j) n -> a (c p) j n", c=2, j=PACK)
+    w_pairs = w.rearrange("(a c) (p j) m -> a (c p) j m", c=2, j=PACK)
+    out_pairs = out.rearrange("(a c) m n -> a m c n", c=2)
+
+    with ExitStack() as ctx:
+        sb = ctx.enter_context(tc.tile_pool(name="sb", bufs=1))
+        ps = ctx.enter_context(tc.psum_pool(name="ps", bufs=1))
+        banks = [[ps.tile([P, 512], F32, name="bank%d_%d" % (c, i)) for i in range(4)] for c in range(2)]
+
+        def operand(name, width):
+            return {
+                "grouped": sb.tile([P, width, PACK], BF16, name=name + "_grouped", align_bytes=64),
+                "codes": sb.tile([P, width], U32, name=name + "_codes", align_bytes=64),
+                "scales": sb.tile([P, width], U8, name=name + "_scales", align_bytes=64),
+            }
+
+        xq = [operand("x%d" % a, N) for a in range(2)]
+        wq = [operand("w%d" % a, M) for a in range(2)]
+        w_raw = [sb.tile([P, PACK, M], F32, name="w_raw%d" % a) for a in range(2)]
+        x_raw = {}
+        relu = [sb.tile([P, 2, N], F32, name="relu%d" % a) for a in range(2)]
+        res = [sb.tile([P, 2, N], F32, name="res%d" % a) for a in range(2)]
+        bias_rows = sb.tile([P, G * QUAD], F32, name="bias_rows", align_bytes=64)
+        bias = sb.tile([P, G * QUAD], F32, name="bias", align_bytes=64)
+        warm = sb.tile([P, 8], F32, name="warm")
+
+        def load_x(a, lo, hi, eng=nc.sync):
+            raw = sb.tile([P, PACK, hi - lo], F32, name="x_raw%d_%d" % (a, lo))
+            eng.dma_start(out=raw[:], in_=x_pairs[a, :, :, lo:hi])
+            for n in range(lo, hi):
+                x_raw[a, n] = (raw, lo)
+
+        def load_w(a, eng=nc.sync):
+            eng.dma_start(out=w_raw[a][:], in_=w_pairs[a])
+
+        def interleave(eng, src, dst):
+            src = src.rearrange("p t (c i) -> p c t i", i=4)
+            dst = dst.rearrange("p (c i) t -> p c t i", i=4)
+            if eng == "V":
+                nc.vector.tensor_copy(out=dst, in_=src)
+            else:
+                nc.scalar.copy(out=dst, in_=src)
+
+        def cast_x(eng, a, lo, hi):
+            raw, base = x_raw[a, lo]
+            interleave(eng, raw[:, :, lo - base : hi - base], xq[a]["grouped"][:, lo:hi, :])
+
+        def cast_w(eng, a, lo=0, hi=M):
+            interleave(eng, w_raw[a][:, :, lo:hi], wq[a]["grouped"][:, lo:hi, :])
+
+        def quant(op, lo, hi):
+            nc.vector.quantize_mx(
+                out=op["codes"][:, lo:hi].bitcast(FP8X4),
+                scales=op["scales"][:, lo:hi],
+                in_=op["grouped"][:, lo:hi, :].rearrange("p n j -> p (n j)"),
+            )
+
+        where = {}
+
+        def mm(a, lo, hi, bank):
+            for n0 in range(lo, hi, N_MM):
+                for c in range(2):
+                    rows = slice(c * ROWS, (c + 1) * ROWS)
+                    cols = slice(n0, n0 + N_MM)
+                    nc.tensor.matmul_mx(
+                        out=banks[c][bank][:, n0 - lo : n0 - lo + N_MM],
+                        lhsT=wq[a]["codes"][rows, :].bitcast(FP8X4),
+                        lhsT_scale=wq[a]["scales"][rows, :],
+                        rhs=xq[a]["codes"][rows, cols].bitcast(FP8X4),
+                        rhs_scale=xq[a]["scales"][rows, cols],
+                        start=True,
+                        stop=True,
+                    )
+            for n in range(lo, hi):
+                where[a, n] = (bank, lo)
+
+        def act(eng, a, c, lo, hi):
+            bank, base = where[a, lo]
+            src = banks[c][bank][:, lo - base : hi - base]
+            g = 2 * a + c
+            col = bias[:, g * QUAD : g * QUAD + 1]
+            if eng == "V":
+                nc.vector.tensor_scalar(
+                    out=relu[a][:, c, lo:hi], in0=src, scalar1=col, scalar2=0.0, op0=ALU.add, op1=ALU.max
+                )
+            else:
+                nc.scalar.activation(out=relu[a][:, c, lo:hi], in_=src, func=ACT.Relu, bias=col)
+
+        def square(eng, a, cs, lo, hi):
+            src = relu[a][:, cs[0] : cs[-1] + 1, lo:hi]
+            dst = res[a][:, cs[0] : cs[-1] + 1, lo:hi]
+            if eng == "V":
+                nc.vector.tensor_tensor(out=dst, in0=src, in1=src, op=ALU.mult)
+            else:
+                nc.scalar.activation(out=dst, in_=src, func=ACT.Square)
+
+        def store(a, cs, lo, hi, eng=nc.sync):
+            eng.dma_start(
+                out=out_pairs[a, :, cs[0] : cs[-1] + 1, lo:hi], in_=res[a][:, cs[0] : cs[-1] + 1, lo:hi]
+            )
+
+        def load_bias(eng):
+            nc.vector.memset(bias_rows[:], 0.0)
+            eng.dma_start(
+                out=bias_rows[0:P:QUAD, :].rearrange("q (g i) -> q g i", g=G),
+                in_=b.rearrange("g (q i) o -> q g (i o)", i=QUAD),
+            )
+
+        def warm_up():
+            nc.vector.memset(warm[:, 0:1], 0.0)
+            nc.scalar.activation(out=warm[:, 1:2], in_=warm[:, 0:1], func=ACT.Relu)
+
+        both = [0, 1]
+        with tc.manual_schedule():
+            load_x(0, 0, 512)
+            load_bias(nc.sync)
+            load_w(0)
+            load_w(1)
+            load_x(1, 0, 256)
+            load_x(1, 256, 384)
+            load_x(1, 384, 512)
+            cast_x("V", 0, 0, 176)
+            cast_x("S", 0, 176, 256)
+            cast_x("S", 0, 256, 384)
+            cast_x("V", 0, 384, 512)
+            quant(xq[0], 0, 256)
+            nc.vector.transpose(out=bias[:], in_=bias_rows[:])
+            cast_w("V", 0)
+            quant(xq[0], 256, 512)
+            quant(wq[0], 0, 128)
+            mm(0, 0, 256, 0)
+            mm(0, 256, 512, 1)
+            cast_w("V", 1)
+            act("S", 0, 0, 0, 256)
+            act("S", 0, 1, 0, 256)
+            act("V", 0, 0, 256, 512)
+            quant(wq[1], 0, 128)
+            square("S", 0, both, 0, 256)
+            cast_x("V", 1, 0, 256)
+            act("S", 0, 1, 256, 512)
+            quant(xq[1], 0, 256)
+            square("S", 0, both, 256, 512)
+            store(0, both, 0, 512)
+            mm(1, 0, 256, 2)
+            cast_x("V", 1, 256, 384)
+            act("S", 1, 0, 0, 256)
+            quant(xq[1], 256, 384)
+            mm(1, 256, 384, 3)
+            act("S", 1, 1, 0, 256)
+            cast_x("V", 1, 384, 512)
+            act("V", 1, 0, 256, 384)
+            quant(xq[1], 384, 512)
+            mm(1, 384, 512, 0)
+            square("S", 1, both, 0, 256)
+            store(1, both, 0, 256)
+            act("V", 1, 1, 256, 384)
+            act("V", 1, 1, 384, 512)
+            square("V", 1, both, 256, 384)
+            store(1, both, 256, 384)
+            act("S", 1, 0, 384, 512)
+            square("S", 1, [0], 384, 512)
+            square("V", 1, [1], 384, 512)
+            store(1, both, 384, 512)

@@ -98,6 +98,21 @@ def tile_rows_glin_relu2_bias_kernel(tc, x, w, b, out):
             for n in range(lo, hi):
                 where[a, n] = (bank, lo)
 
+        def mm1(a, c, n0, bank):
+            rows = slice(c * ROWS, (c + 1) * ROWS)
+            cols = slice(n0, n0 + N_MM)
+            nc.tensor.matmul_mx(
+                out=banks[c][bank][:, cols],
+                lhsT=wq[a]["codes"][rows, :].bitcast(FP8X4),
+                lhsT_scale=wq[a]["scales"][rows, :],
+                rhs=xq[a]["codes"][rows, cols].bitcast(FP8X4),
+                rhs_scale=xq[a]["scales"][rows, cols],
+                start=True,
+                stop=True,
+            )
+            for n in range(n0, n0 + N_MM):
+                where[a, n] = (bank, 0)
+
         def act(eng, a, c, lo, hi):
             bank, base = where[a, lo]
             src = banks[c][bank][:, lo - base : hi - base]
@@ -136,52 +151,66 @@ def tile_rows_glin_relu2_bias_kernel(tc, x, w, b, out):
 
         both = [0, 1]
         with tc.manual_schedule():
+            bank_of = [0,0,1,1,2,2,3,0]
             load_x(0, 0, 512)
-            load_bias(nc.sync)
             load_w(0)
+            load_bias(nc.sync)
             load_w(1)
             load_x(1, 0, 256)
-            load_x(1, 256, 384)
-            load_x(1, 384, 512)
-            cast_x("V", 0, 0, 176)
-            cast_x("S", 0, 176, 256)
-            cast_x("S", 0, 256, 384)
-            cast_x("V", 0, 384, 512)
+            load_x(1, 256, 512)
+            cast_x("S", 0, 0, 128)
+            cast_x("V", 0, 128, 352)
+            cast_w("V", 0, 0, 128)
             quant(xq[0], 0, 256)
-            nc.vector.transpose(out=bias[:], in_=bias_rows[:])
-            cast_w("V", 0)
-            quant(xq[0], 256, 512)
             quant(wq[0], 0, 128)
-            mm(0, 0, 256, 0)
-            mm(0, 256, 512, 1)
-            cast_w("V", 1)
+            mm1(0, 0, 0, bank_of[0])
+            mm1(0, 0, 128, bank_of[1])
+            mm1(0, 1, 0, bank_of[0])
+            mm1(0, 1, 128, bank_of[1])
+            cast_x("S", 0, 352, 512)
+            cast_w("S", 1, 0, 128)
+            nc.vector.transpose(out=bias[:], in_=bias_rows[:])
+            quant(xq[0], 256, 512)
+            mm1(0, 0, 256, bank_of[2])
+            mm1(0, 0, 384, bank_of[3])
+            mm1(0, 1, 256, bank_of[2])
+            mm1(0, 1, 384, bank_of[3])
+            quant(wq[1], 0, 128)
             act("S", 0, 0, 0, 256)
             act("S", 0, 1, 0, 256)
-            act("V", 0, 0, 256, 512)
-            quant(wq[1], 0, 128)
-            square("S", 0, both, 0, 256)
-            cast_x("V", 1, 0, 256)
+            act("S", 0, 0, 256, 512)
             act("S", 0, 1, 256, 512)
+            cast_x("V", 1, 0, 256)
             quant(xq[1], 0, 256)
-            square("S", 0, both, 256, 512)
-            store(0, both, 0, 512)
-            mm(1, 0, 256, 2)
+            mm1(1, 0, 0, bank_of[4])
+            mm1(1, 0, 128, bank_of[5])
+            mm1(1, 1, 0, bank_of[4])
+            mm1(1, 1, 128, bank_of[5])
+            square("S", 0, [0], 0, 512)
+            store(0, [0], 0, 512, nc.sync)
+            square("S", 0, [1], 0, 512)
+            store(0, [1], 0, 512, nc.sync)
             cast_x("V", 1, 256, 384)
-            act("S", 1, 0, 0, 256)
-            quant(xq[1], 256, 384)
-            mm(1, 256, 384, 3)
-            act("S", 1, 1, 0, 256)
             cast_x("V", 1, 384, 512)
-            act("V", 1, 0, 256, 384)
+            quant(xq[1], 256, 384)
             quant(xq[1], 384, 512)
-            mm(1, 384, 512, 0)
-            square("S", 1, both, 0, 256)
-            store(1, both, 0, 256)
-            act("V", 1, 1, 256, 384)
-            act("V", 1, 1, 384, 512)
-            square("V", 1, both, 256, 384)
-            store(1, both, 256, 384)
-            act("S", 1, 0, 384, 512)
-            square("S", 1, [0], 384, 512)
-            square("V", 1, [1], 384, 512)
-            store(1, both, 384, 512)
+            mm1(1, 0, 256, bank_of[6])
+            mm1(1, 1, 256, bank_of[6])
+            mm1(1, 0, 384, bank_of[7])
+            mm1(1, 1, 384, bank_of[7])
+            act("S", 1, 0, 0, 256)
+            act("V", 1, 1, 0, 256)
+            square("V", 1, [0], 0, 256)
+            store(1, [0], 0, 256, nc.sync)
+            square("S", 1, [1], 0, 256)
+            store(1, [1], 0, 256, nc.sync)
+            act("S", 1, 1, 256, 384)
+            act("V", 1, 0, 256, 384)
+            act("V", 1, 0, 384, 512)
+            act("S", 1, 1, 384, 512)
+            square("V", 1, [0], 256, 384)
+            square("V", 1, [0], 384, 512)
+            store(1, [0], 256, 512, nc.sync)
+            square("S", 1, [1], 256, 384)
+            square("S", 1, [1], 384, 512)
+            store(1, [1], 256, 512, nc.scalar)

@@ -158,8 +158,8 @@ def tile_rows_glin_relu2_bias_kernel(tc, x, w, b, out):
             load_w(1)
             load_x(1, 0, 256)
             load_x(1, 256, 512)
-            cast_x("S", 0, 0, 128)
-            cast_x("V", 0, 128, 352)
+            cast_x("V", 0, 0, 256)
+            cast_x("S", 0, 256, 512)
             cast_w("V", 0, 0, 128)
             quant(xq[0], 0, 256)
             quant(wq[0], 0, 128)
@@ -167,20 +167,19 @@ def tile_rows_glin_relu2_bias_kernel(tc, x, w, b, out):
             mm1(0, 0, 128, bank_of[1])
             mm1(0, 1, 0, bank_of[0])
             mm1(0, 1, 128, bank_of[1])
-            cast_x("S", 0, 352, 512)
             cast_w("S", 1, 0, 128)
-            nc.vector.transpose(out=bias[:], in_=bias_rows[:])
             quant(xq[0], 256, 512)
             mm1(0, 0, 256, bank_of[2])
             mm1(0, 0, 384, bank_of[3])
             mm1(0, 1, 256, bank_of[2])
             mm1(0, 1, 384, bank_of[3])
+            nc.vector.transpose(out=bias[:], in_=bias_rows[:])
             quant(wq[1], 0, 128)
             act("S", 0, 0, 0, 256)
-            act("S", 0, 1, 0, 256)
             act("S", 0, 0, 256, 512)
-            act("S", 0, 1, 256, 512)
             cast_x("V", 1, 0, 256)
+            act("V", 0, 1, 0, 256)
+            act("S", 0, 1, 256, 512)
             quant(xq[1], 0, 256)
             mm1(1, 0, 0, bank_of[4])
             mm1(1, 0, 128, bank_of[5])
@@ -199,13 +198,13 @@ def tile_rows_glin_relu2_bias_kernel(tc, x, w, b, out):
             mm1(1, 0, 384, bank_of[7])
             mm1(1, 1, 384, bank_of[7])
             act("S", 1, 0, 0, 256)
-            act("V", 1, 1, 0, 256)
+            act("S", 1, 1, 0, 256)
             square("V", 1, [0], 0, 256)
             store(1, [0], 0, 256, nc.sync)
             square("S", 1, [1], 0, 256)
             store(1, [1], 0, 256, nc.sync)
-            act("S", 1, 1, 256, 384)
             act("V", 1, 0, 256, 384)
+            act("S", 1, 1, 256, 384)
             act("V", 1, 0, 384, 512)
             act("S", 1, 1, 384, 512)
             square("V", 1, [0], 256, 384)

@@ -152,14 +152,14 @@ def tile_rows_glin_relu2_bias_kernel(tc, x, w, b, out):
         both = [0, 1]
         with tc.manual_schedule():
             bank_of = [0,0,1,1,2,2,3,0]
-            load_x(0, 0, 512)
+            load_x(0, 0, 256)
             load_w(0)
             load_bias(nc.sync)
+            load_x(0, 256, 512)
             load_w(1)
             load_x(1, 0, 256)
             load_x(1, 256, 512)
             cast_x("V", 0, 0, 256)
-            cast_x("S", 0, 256, 512)
             cast_w("V", 0, 0, 128)
             quant(xq[0], 0, 256)
             quant(wq[0], 0, 128)
@@ -167,25 +167,30 @@ def tile_rows_glin_relu2_bias_kernel(tc, x, w, b, out):
             mm1(0, 0, 128, bank_of[1])
             mm1(0, 1, 0, bank_of[0])
             mm1(0, 1, 128, bank_of[1])
-            cast_w("S", 1, 0, 128)
+            nc.vector.transpose(out=bias[:], in_=bias_rows[:])
+            cast_x("V", 0, 256, 416)
+            cast_x("S", 0, 416, 512)
+            act("S", 0, 0, 0, 256)
+            act("S", 0, 1, 0, 256)
             quant(xq[0], 256, 512)
             mm1(0, 0, 256, bank_of[2])
             mm1(0, 0, 384, bank_of[3])
             mm1(0, 1, 256, bank_of[2])
             mm1(0, 1, 384, bank_of[3])
-            nc.vector.transpose(out=bias[:], in_=bias_rows[:])
-            quant(wq[1], 0, 128)
-            act("S", 0, 0, 0, 256)
+            cast_w("V", 1, 0, 128)
+            square("S", 0, [0], 0, 256)
             act("S", 0, 0, 256, 512)
-            cast_x("V", 1, 0, 256)
-            act("V", 0, 1, 0, 256)
             act("S", 0, 1, 256, 512)
-            quant(xq[1], 0, 256)
+            quant(wq[1], 0, 128)
+            cast_x("V", 1, 0, 128)
+            cast_x("V", 1, 128, 256)
+            quant(xq[1], 0, 128)
+            quant(xq[1], 128, 256)
             mm1(1, 0, 0, bank_of[4])
-            mm1(1, 0, 128, bank_of[5])
             mm1(1, 1, 0, bank_of[4])
+            mm1(1, 0, 128, bank_of[5])
             mm1(1, 1, 128, bank_of[5])
-            square("S", 0, [0], 0, 512)
+            square("S", 0, [0], 256, 512)
             store(0, [0], 0, 512, nc.sync)
             square("S", 0, [1], 0, 512)
             store(0, [1], 0, 512, nc.sync)
@@ -199,17 +204,16 @@ def tile_rows_glin_relu2_bias_kernel(tc, x, w, b, out):
             mm1(1, 1, 384, bank_of[7])
             act("S", 1, 0, 0, 256)
             act("S", 1, 1, 0, 256)
-            square("V", 1, [0], 0, 256)
+            square("S", 1, [0], 0, 256)
             store(1, [0], 0, 256, nc.sync)
-            square("S", 1, [1], 0, 256)
+            square("V", 1, [1], 0, 256)
             store(1, [1], 0, 256, nc.sync)
-            act("V", 1, 0, 256, 384)
             act("S", 1, 1, 256, 384)
-            act("V", 1, 0, 384, 512)
+            act("V", 1, 0, 256, 384)
             act("S", 1, 1, 384, 512)
-            square("V", 1, [0], 256, 384)
+            act("V", 1, 0, 384, 512)
+            square("S", 1, [0,1], 256, 384)
+            store(1, [0,1], 256, 384, nc.sync)
             square("V", 1, [0], 384, 512)
-            store(1, [0], 256, 512, nc.sync)
-            square("S", 1, [1], 256, 384)
             square("S", 1, [1], 384, 512)
-            store(1, [1], 256, 512, nc.scalar)
+            store(1, [0,1], 384, 512, nc.sync)

@@ -46,7 +46,6 @@ def tile_rows_glin_relu2_bias_kernel(tc, x, w, b, out):
         res = [sb.tile([P, 2, N], F32, name="res%d" % a) for a in range(2)]
         bias_rows = sb.tile([P, G * QUAD], F32, name="bias_rows", align_bytes=64)
         bias = sb.tile([P, G * QUAD], F32, name="bias", align_bytes=64)
-        warm = sb.tile([P, 8], F32, name="warm")
 
         def load_x(a, lo, hi, eng=nc.sync):
             raw = sb.tile([P, PACK, hi - lo], F32, name="x_raw%d_%d" % (a, lo))
@@ -81,13 +80,13 @@ def tile_rows_glin_relu2_bias_kernel(tc, x, w, b, out):
 
         where = {}
 
-        def mm(a, lo, hi, bank):
+        def mm(a, lo, hi, bank, cs=(0, 1)):
             for n0 in range(lo, hi, N_MM):
-                for c in range(2):
+                for c in cs:
                     rows = slice(c * ROWS, (c + 1) * ROWS)
                     cols = slice(n0, n0 + N_MM)
                     nc.tensor.matmul_mx(
-                        out=banks[c][bank][:, n0 - lo : n0 - lo + N_MM],
+                        out=banks[c][bank][:, cols],
                         lhsT=wq[a]["codes"][rows, :].bitcast(FP8X4),
                         lhsT_scale=wq[a]["scales"][rows, :],
                         rhs=xq[a]["codes"][rows, cols].bitcast(FP8X4),
@@ -96,26 +95,10 @@ def tile_rows_glin_relu2_bias_kernel(tc, x, w, b, out):
                         stop=True,
                     )
             for n in range(lo, hi):
-                where[a, n] = (bank, lo)
-
-        def mm1(a, c, n0, bank):
-            rows = slice(c * ROWS, (c + 1) * ROWS)
-            cols = slice(n0, n0 + N_MM)
-            nc.tensor.matmul_mx(
-                out=banks[c][bank][:, cols],
-                lhsT=wq[a]["codes"][rows, :].bitcast(FP8X4),
-                lhsT_scale=wq[a]["scales"][rows, :],
-                rhs=xq[a]["codes"][rows, cols].bitcast(FP8X4),
-                rhs_scale=xq[a]["scales"][rows, cols],
-                start=True,
-                stop=True,
-            )
-            for n in range(n0, n0 + N_MM):
-                where[a, n] = (bank, 0)
+                where[a, n] = bank
 
         def act(eng, a, c, lo, hi):
-            bank, base = where[a, lo]
-            src = banks[c][bank][:, lo - base : hi - base]
+            src = banks[c][where[a, lo]][:, lo:hi]
             g = 2 * a + c
             col = bias[:, g * QUAD : g * QUAD + 1]
             if eng == "V":
@@ -130,6 +113,8 @@ def tile_rows_glin_relu2_bias_kernel(tc, x, w, b, out):
             dst = res[a][:, cs[0] : cs[-1] + 1, lo:hi]
             if eng == "V":
                 nc.vector.tensor_tensor(out=dst, in0=src, in1=src, op=ALU.mult)
+            elif eng == "G":
+                nc.gpsimd.tensor_tensor(out=dst, in0=src, in1=src, op=ALU.mult)
             else:
                 nc.scalar.activation(out=dst, in_=src, func=ACT.Square)
 
@@ -145,13 +130,10 @@ def tile_rows_glin_relu2_bias_kernel(tc, x, w, b, out):
                 in_=b.rearrange("g (q i) o -> q g (i o)", i=QUAD),
             )
 
-        def warm_up():
-            nc.vector.memset(warm[:, 0:1], 0.0)
-            nc.scalar.activation(out=warm[:, 1:2], in_=warm[:, 0:1], func=ACT.Relu)
+        def turn_bias():
+            nc.vector.transpose(out=bias[:], in_=bias_rows[:])
 
-        both = [0, 1]
         with tc.manual_schedule():
-            bank_of = [0,0,1,1,2,2,3,0]
             load_x(0, 0, 256)
             load_w(0)
             load_bias(nc.sync)
@@ -159,61 +141,57 @@ def tile_rows_glin_relu2_bias_kernel(tc, x, w, b, out):
             load_w(1)
             load_x(1, 0, 256)
             load_x(1, 256, 512)
-            cast_x("V", 0, 0, 256)
-            cast_w("V", 0, 0, 128)
+            cast_x("V", 0, 0, 160)
+            cast_x("S", 0, 160, 256)
+            cast_w("V", 0, 0, 64)
+            cast_w("S", 0, 64, 128)
             quant(xq[0], 0, 256)
             quant(wq[0], 0, 128)
-            mm1(0, 0, 0, bank_of[0])
-            mm1(0, 0, 128, bank_of[1])
-            mm1(0, 1, 0, bank_of[0])
-            mm1(0, 1, 128, bank_of[1])
-            nc.vector.transpose(out=bias[:], in_=bias_rows[:])
+            mm(0, 0, 256, 0)
+            turn_bias()
             cast_x("V", 0, 256, 416)
             cast_x("S", 0, 416, 512)
+            quant(xq[0], 256, 512)
+            mm(0, 256, 512, 1)
             act("S", 0, 0, 0, 256)
             act("S", 0, 1, 0, 256)
-            quant(xq[0], 256, 512)
-            mm1(0, 0, 256, bank_of[2])
-            mm1(0, 0, 384, bank_of[3])
-            mm1(0, 1, 256, bank_of[2])
-            mm1(0, 1, 384, bank_of[3])
-            cast_w("V", 1, 0, 128)
-            square("S", 0, [0], 0, 256)
-            act("S", 0, 0, 256, 512)
-            act("S", 0, 1, 256, 512)
+            cast_w("V", 1)
+            square("V", 0, [0], 0, 256)
             quant(wq[1], 0, 128)
+            square("S", 0, [1], 0, 256)
             cast_x("V", 1, 0, 128)
             cast_x("V", 1, 128, 256)
             quant(xq[1], 0, 128)
+            mm(1, 0, 128, 2)
             quant(xq[1], 128, 256)
-            mm1(1, 0, 0, bank_of[4])
-            mm1(1, 1, 0, bank_of[4])
-            mm1(1, 0, 128, bank_of[5])
-            mm1(1, 1, 128, bank_of[5])
+            mm(1, 128, 256, 3)
+            act("S", 0, 0, 256, 512)
+            act("S", 0, 1, 256, 512)
             square("S", 0, [0], 256, 512)
-            store(0, [0], 0, 512, nc.sync)
-            square("S", 0, [1], 0, 512)
-            store(0, [1], 0, 512, nc.sync)
+            store(0, [0], 0, 512)
+            square("S", 0, [1], 256, 512)
+            store(0, [1], 0, 512)
+
             cast_x("V", 1, 256, 384)
-            cast_x("V", 1, 384, 512)
+            cast_x("V", 1, 384, 456)
+            cast_x("S", 1, 456, 512)
             quant(xq[1], 256, 384)
+            mm(1, 256, 384, 0)
             quant(xq[1], 384, 512)
-            mm1(1, 0, 256, bank_of[6])
-            mm1(1, 1, 256, bank_of[6])
-            mm1(1, 0, 384, bank_of[7])
-            mm1(1, 1, 384, bank_of[7])
-            act("S", 1, 0, 0, 256)
-            act("S", 1, 1, 0, 256)
+            mm(1, 384, 512, 1)
+            act("S", 1, 1, 0, 128)
+            act("S", 1, 0, 0, 128)
+            act("S", 1, 1, 128, 256)
+            act("S", 1, 0, 128, 256)
+            square("V", 1, [1], 0, 128)
+            square("V", 1, [1], 128, 256)
+            store(1, [1], 0, 256)
             square("S", 1, [0], 0, 256)
-            store(1, [0], 0, 256, nc.sync)
-            square("V", 1, [1], 0, 256)
-            store(1, [1], 0, 256, nc.sync)
-            act("S", 1, 1, 256, 384)
-            act("V", 1, 0, 256, 384)
-            act("S", 1, 1, 384, 512)
-            act("V", 1, 0, 384, 512)
-            square("S", 1, [0,1], 256, 384)
-            store(1, [0,1], 256, 384, nc.sync)
-            square("V", 1, [0], 384, 512)
-            square("S", 1, [1], 384, 512)
-            store(1, [0,1], 384, 512, nc.sync)
+            store(1, [0], 0, 256)
+            for lo in (256, 384):
+                act("S", 1, 0, lo, lo + 128)
+                act("V", 1, 1, lo, lo + 128)
+            for lo in (256, 384):
+                square("S", 1, [0], lo, lo + 128)
+                square("V", 1, [1], lo, lo + 128)
+                store(1, [0, 1], lo, lo + 128)

@@ -40,15 +40,15 @@ def tile_rows_glin_relu2_bias_kernel(tc, x, w, b, out):
 
         xq = [operand("x%d" % a, N) for a in range(2)]
         wq = [operand("w%d" % a, M) for a in range(2)]
-        w_raw = [sb.tile([P, PACK, M], F32, name="w_raw%d" % a) for a in range(2)]
+        w_raw = [sb.tile([P, PACK, M], F32, name="w_raw%d" % a, align_bytes=256) for a in range(2)]
         x_raw = {}
         relu = [sb.tile([P, 2, N], F32, name="relu%d" % a) for a in range(2)]
-        res = [sb.tile([P, 2, N], F32, name="res%d" % a) for a in range(2)]
+        res = [sb.tile([P, 2, N], F32, name="res%d" % a, align_bytes=256) for a in range(2)]
         bias_rows = sb.tile([P, G * QUAD], F32, name="bias_rows", align_bytes=64)
         bias = sb.tile([P, G * QUAD], F32, name="bias", align_bytes=64)
 
         def load_x(a, lo, hi, eng=nc.sync):
-            raw = sb.tile([P, PACK, hi - lo], F32, name="x_raw%d_%d" % (a, lo))
+            raw = sb.tile([P, PACK, hi - lo], F32, name="x_raw%d_%d" % (a, lo), align_bytes=256)
             eng.dma_start(out=raw[:], in_=x_pairs[a, :, :, lo:hi])
             for n in range(lo, hi):
                 x_raw[a, n] = (raw, lo)

@@ -138,56 +138,60 @@ def tile_rows_glin_relu2_bias_kernel(tc, x, w, b, out):
             load_w(0)
             load_bias(nc.sync)
             load_x(0, 256, 512)
-            load_w(1)
             load_x(1, 0, 256)
+            load_w(1)
             load_x(1, 256, 512)
-            cast_x("V", 0, 0, 160)
-            cast_x("S", 0, 160, 256)
-            cast_w("V", 0, 0, 64)
-            cast_w("S", 0, 64, 128)
+            cast_x("V", 0, 0, 168)
+            cast_x("S", 0, 168, 256)
+            cast_w("V", 0, 0, 88)
+            cast_w("S", 0, 88, 128)
             quant(xq[0], 0, 256)
             quant(wq[0], 0, 128)
-            mm(0, 0, 256, 0)
+            mm(0, 0, 128, 0)
+            mm(0, 128, 256, 1)
             turn_bias()
-            cast_x("V", 0, 256, 416)
-            cast_x("S", 0, 416, 512)
-            quant(xq[0], 256, 512)
-            mm(0, 256, 512, 1)
-            act("S", 0, 0, 0, 256)
-            act("S", 0, 1, 0, 256)
+            cast_x("V", 0, 256, 384)
+            cast_x("V", 0, 384, 512)
+            quant(xq[0], 256, 384)
+            mm(0, 256, 384, 2)
+            act("S", 0, 0, 0, 128)
+            act("S", 0, 1, 0, 128)
+            act("S", 0, 0, 128, 256)
+            act("V", 0, 1, 128, 256)
+            quant(xq[0], 384, 512)
+            mm(0, 384, 512, 3)
+            square("S", 0, [0, 1], 0, 128)
+            square("S", 0, [0, 1], 128, 256)
+            store(0, [0, 1], 0, 256)
+            cast_x("V", 1, 0, 256)
             cast_w("V", 1)
-            square("V", 0, [0], 0, 256)
+            quant(xq[1], 0, 256)
             quant(wq[1], 0, 128)
-            square("S", 0, [1], 0, 256)
-            cast_x("V", 1, 0, 128)
-            cast_x("V", 1, 128, 256)
-            quant(xq[1], 0, 128)
-            mm(1, 0, 128, 2)
-            quant(xq[1], 128, 256)
-            mm(1, 128, 256, 3)
-            act("S", 0, 0, 256, 512)
-            act("S", 0, 1, 256, 512)
-            square("S", 0, [0], 256, 512)
-            store(0, [0], 0, 512)
-            square("S", 0, [1], 256, 512)
-            store(0, [1], 0, 512)
-
-            cast_x("V", 1, 256, 384)
-            cast_x("V", 1, 384, 456)
-            cast_x("S", 1, 456, 512)
+            mm(1, 0, 128, 0)
+            mm(1, 128, 256, 1)
+            act("S", 0, 0, 256, 384)
+            act("S", 0, 1, 256, 384)
+            act("S", 0, 0, 384, 512)
+            act("S", 0, 1, 384, 512)
+            square("V", 0, [0, 1], 256, 384)
+            square("S", 0, [0, 1], 384, 512)
+            store(0, [0, 1], 256, 512)
+            cast_x("V", 1, 256, 344)
+            cast_x("S", 1, 344, 384)
+            cast_x("V", 1, 384, 472)
+            cast_x("S", 1, 472, 512)
             quant(xq[1], 256, 384)
-            mm(1, 256, 384, 0)
+            mm(1, 256, 384, 2)
             quant(xq[1], 384, 512)
-            mm(1, 384, 512, 1)
-            act("S", 1, 1, 0, 128)
+            mm(1, 384, 512, 3)
             act("S", 1, 0, 0, 128)
-            act("S", 1, 1, 128, 256)
+            act("S", 1, 1, 0, 128)
+            act("V", 1, 1, 128, 256)
             act("S", 1, 0, 128, 256)
-            square("V", 1, [1], 0, 128)
-            square("V", 1, [1], 128, 256)
-            store(1, [1], 0, 256)
-            square("S", 1, [0], 0, 256)
-            store(1, [0], 0, 256)
+            for lo in (0, 128):
+                square("V", 1, [1], lo, lo + 128)
+                square("S", 1, [0], lo, lo + 128)
+            store(1, [0, 1], 0, 256)
             for lo in (256, 384):
                 act("S", 1, 0, lo, lo + 128)
                 act("V", 1, 1, lo, lo + 128)

@@ -198,4 +198,4 @@ def tile_rows_glin_relu2_bias_kernel(tc, x, w, b, out):
             for lo in (256, 384):
                 square("S", 1, [0], lo, lo + 128)
                 square("V", 1, [1], lo, lo + 128)
-                store(1, [0, 1], lo, lo + 128)
+            store(1, [0, 1], 256, 512)

@@ -148,7 +148,7 @@ def tile_rows_glin_relu2_bias_kernel(tc, x, w, b, out):
             quant(xq[0], 0, 256)
             quant(wq[0], 0, 128)
             mm(0, 0, 128, 0)
-            mm(0, 128, 256, 1)
+            mm(0, 128, 256, 1, (1, 0))
             turn_bias()
             cast_x("V", 0, 256, 384)
             cast_x("V", 0, 384, 512)
@@ -159,7 +159,7 @@ def tile_rows_glin_relu2_bias_kernel(tc, x, w, b, out):
             act("S", 0, 0, 128, 256)
             act("V", 0, 1, 128, 256)
             quant(xq[0], 384, 512)
-            mm(0, 384, 512, 3)
+            mm(0, 384, 512, 3, (1, 0))
             square("S", 0, [0, 1], 0, 128)
             square("S", 0, [0, 1], 128, 256)
             store(0, [0, 1], 0, 256)
@@ -168,7 +168,7 @@ def tile_rows_glin_relu2_bias_kernel(tc, x, w, b, out):
             quant(xq[1], 0, 256)
             quant(wq[1], 0, 128)
             mm(1, 0, 128, 0)
-            mm(1, 128, 256, 1)
+            mm(1, 128, 256, 1, (1, 0))
             act("S", 0, 0, 256, 384)
             act("S", 0, 1, 256, 384)
             act("S", 0, 0, 384, 512)
@@ -183,7 +183,7 @@ def tile_rows_glin_relu2_bias_kernel(tc, x, w, b, out):
             quant(xq[1], 256, 384)
             mm(1, 256, 384, 2)
             quant(xq[1], 384, 512)
-            mm(1, 384, 512, 3)
+            mm(1, 384, 512, 3, (1, 0))
             act("S", 1, 0, 0, 128)
             act("S", 1, 1, 0, 128)
             act("V", 1, 1, 128, 256)

@@ -57,8 +57,8 @@ def tile_rows_glin_relu2_bias_kernel(tc, x, w, b, out):
             eng.dma_start(out=w_raw[a][:], in_=w_pairs[a])
 
         def interleave(eng, src, dst):
-            src = src.rearrange("p t (c i) -> p c t i", i=4)
-            dst = dst.rearrange("p (c i) t -> p c t i", i=4)
+            src = src.rearrange("p t (c i) -> p c t i", i=2)
+            dst = dst.rearrange("p (c i) t -> p c t i", i=2)
             if eng == "V":
                 nc.vector.tensor_copy(out=dst, in_=src)
             else:

@@ -191,11 +191,13 @@ def tile_rows_glin_relu2_bias_kernel(tc, x, w, b, out):
             for lo in (0, 128):
                 square("V", 1, [1], lo, lo + 128)
                 square("S", 1, [0], lo, lo + 128)
-            store(1, [0, 1], 0, 256)
+            store(1, [1], 0, 256)
+            store(1, [0], 0, 256)
             for lo in (256, 384):
                 act("S", 1, 0, lo, lo + 128)
                 act("V", 1, 1, lo, lo + 128)
             for lo in (256, 384):
                 square("S", 1, [0], lo, lo + 128)
                 square("V", 1, [1], lo, lo + 128)
-            store(1, [0, 1], 256, 512)
+            store(1, [1], 256, 512)
+            store(1, [0], 256, 512)

@@ -162,7 +162,8 @@ def tile_rows_glin_relu2_bias_kernel(tc, x, w, b, out):
             mm(0, 384, 512, 3, (1, 0))
             square("S", 0, [0, 1], 0, 128)
             square("S", 0, [0, 1], 128, 256)
-            store(0, [0, 1], 0, 256)
+            store(0, [0], 0, 256)
+            store(0, [1], 0, 256)
             cast_x("V", 1, 0, 256)
             cast_w("V", 1)
             quant(xq[1], 0, 256)
@@ -173,14 +174,15 @@ def tile_rows_glin_relu2_bias_kernel(tc, x, w, b, out):
             act("S", 0, 1, 256, 384)
             act("S", 0, 0, 384, 512)
             act("S", 0, 1, 384, 512)
-            square("V", 0, [0, 1], 256, 384)
-            square("S", 0, [0, 1], 384, 512)
-            store(0, [0, 1], 256, 512)
-            cast_x("V", 1, 256, 344)
-            cast_x("S", 1, 344, 384)
-            cast_x("V", 1, 384, 472)
-            cast_x("S", 1, 472, 512)
-            quant(xq[1], 256, 384)
+            square("S", 0, [0], 256, 512)
+            store(0, [0], 256, 512)
+            square("V", 0, [1], 256, 512)
+            store(0, [1], 256, 512)
+            cast_x("V", 1, 256, 320)
+            cast_x("S", 1, 320, 384)
+            cast_x("V", 1, 384, 512)
+            quant(xq[1], 256, 320)
+            quant(xq[1], 320, 384)
             mm(1, 256, 384, 2)
             quant(xq[1], 384, 512)
             mm(1, 384, 512, 3, (1, 0))

@@ -166,34 +166,40 @@ def tile_rows_glin_relu2_bias_kernel(tc, x, w, b, out):
             store(0, [1], 0, 256)
             cast_x("V", 1, 0, 256)
             cast_w("V", 1)
-            quant(xq[1], 0, 256)
-            quant(wq[1], 0, 128)
-            mm(1, 0, 128, 0)
-            mm(1, 128, 256, 1, (1, 0))
-            act("S", 0, 0, 256, 384)
             act("S", 0, 1, 256, 384)
+            act("S", 0, 0, 256, 384)
             act("S", 0, 0, 384, 512)
             act("S", 0, 1, 384, 512)
+            quant(xq[1], 0, 128)
+            square("V", 0, [1], 256, 320)
+            quant(wq[1], 0, 128)
+            mm(1, 0, 128, 0, (0, 1))
+            quant(xq[1], 128, 256)
+            mm(1, 128, 256, 1, (1, 0))
             square("S", 0, [0], 256, 512)
             store(0, [0], 256, 512)
-            square("V", 0, [1], 256, 512)
+            square("V", 0, [1], 320, 384)
+            square("S", 0, [1], 384, 512)
             store(0, [1], 256, 512)
             cast_x("V", 1, 256, 320)
             cast_x("S", 1, 320, 384)
             cast_x("V", 1, 384, 512)
             quant(xq[1], 256, 320)
             quant(xq[1], 320, 384)
-            mm(1, 256, 384, 2)
+            mm(1, 256, 384, 2, (1,))
             quant(xq[1], 384, 512)
-            mm(1, 384, 512, 3, (1, 0))
-            act("S", 1, 0, 0, 128)
+            mm(1, 384, 512, 3, (1,))
+            mm(1, 256, 384, 2, (0,))
+            mm(1, 384, 512, 3, (0,))
             act("S", 1, 1, 0, 128)
-            act("V", 1, 1, 128, 256)
+            act("S", 1, 1, 128, 256)
+            act("S", 1, 0, 0, 128)
             act("S", 1, 0, 128, 256)
             for lo in (0, 128):
                 square("V", 1, [1], lo, lo + 128)
-                square("S", 1, [0], lo, lo + 128)
             store(1, [1], 0, 256)
+            square("S", 1, [0], 0, 128)
+            square("S", 1, [0], 128, 256)
             store(1, [0], 0, 256)
             for lo in (256, 384):
                 act("S", 1, 0, lo, lo + 128)

from contextlib import ExitStack

import concourse.mybir as mybir

G, D, M, N = 4, 256, 128, 512
FLOPS = 2 * G * D * M * N

F32 = mybir.dt.float32
BF16 = mybir.dt.bfloat16
U32 = mybir.dt.uint32
U8 = mybir.dt.uint8
FP8X4 = mybir.dt.float8_e4m3fn_x4
ALU = mybir.AluOpType
ACT = mybir.ActivationFunctionType

P = 128
PACK = 4
ROWS = D // PACK
N_MM = 128
QUAD = 32


def tile_rows_glin_relu2_bias_kernel(tc, x, w, b, out):
    nc = tc.nc
    x_pairs = x.rearrange("(a c) (p j) n -> a (c p) j n", c=2, j=PACK)
    w_pairs = w.rearrange("(a c) (p j) m -> a (c p) j m", c=2, j=PACK)
    out_pairs = out.rearrange("(a c) m n -> a m c n", c=2)

    with ExitStack() as ctx:
        sb = ctx.enter_context(tc.tile_pool(name="sb", bufs=1))
        ps = ctx.enter_context(tc.psum_pool(name="ps", bufs=1))
        banks = [[ps.tile([P, 512], F32, name="bank%d_%d" % (c, i)) for i in range(4)] for c in range(2)]

        def operand(name, width):
            return {
                "grouped": sb.tile([P, width, PACK], BF16, name=name + "_grouped", align_bytes=64),
                "codes": sb.tile([P, width], U32, name=name + "_codes", align_bytes=64),
                "scales": sb.tile([P, width], U8, name=name + "_scales", align_bytes=64),
            }

        xq = [operand("x%d" % a, N) for a in range(2)]
        wq = [operand("w%d" % a, M) for a in range(2)]
        w_raw = [sb.tile([P, PACK, M], F32, name="w_raw%d" % a, align_bytes=256) for a in range(2)]
        x_raw = {}
        relu = [sb.tile([P, 2, N], F32, name="relu%d" % a) for a in range(2)]
        res = [sb.tile([P, 2, N], F32, name="res%d" % a, align_bytes=256) for a in range(2)]
        bias_rows = sb.tile([P, G * QUAD], F32, name="bias_rows", align_bytes=64)
        bias = sb.tile([P, G * QUAD], F32, name="bias", align_bytes=64)

        def load_x(a, lo, hi, eng=nc.sync):
            raw = sb.tile([P, PACK, hi - lo], F32, name="x_raw%d_%d" % (a, lo), align_bytes=256)
            eng.dma_start(out=raw[:], in_=x_pairs[a, :, :, lo:hi])
            for n in range(lo, hi):
                x_raw[a, n] = (raw, lo)

        def load_w(a, eng=nc.sync):
            eng.dma_start(out=w_raw[a][:], in_=w_pairs[a])

        def interleave(eng, src, dst):
            src = src.rearrange("p t (c i) -> p c t i", i=2)
            dst = dst.rearrange("p (c i) t -> p c t i", i=2)
            if eng == "V":
                nc.vector.tensor_copy(out=dst, in_=src)
            else:
                nc.scalar.copy(out=dst, in_=src)

        def cast_x(eng, a, lo, hi):
            raw, base = x_raw[a, lo]
            interleave(eng, raw[:, :, lo - base : hi - base], xq[a]["grouped"][:, lo:hi, :])

        def cast_w(eng, a, lo=0, hi=M):
            interleave(eng, w_raw[a][:, :, lo:hi], wq[a]["grouped"][:, lo:hi, :])

        def quant(op, lo, hi):
            nc.vector.quantize_mx(
                out=op["codes"][:, lo:hi].bitcast(FP8X4),
                scales=op["scales"][:, lo:hi],
                in_=op["grouped"][:, lo:hi, :].rearrange("p n j -> p (n j)"),
            )

        where = {}

        def mm(a, lo, hi, bank, cs=(0, 1)):
            for n0 in range(lo, hi, N_MM):
                for c in cs:
                    rows = slice(c * ROWS, (c + 1) * ROWS)
                    cols = slice(n0, n0 + N_MM)
                    nc.tensor.matmul_mx(
                        out=banks[c][bank][:, cols],
                        lhsT=wq[a]["codes"][rows, :].bitcast(FP8X4),
                        lhsT_scale=wq[a]["scales"][rows, :],
                        rhs=xq[a]["codes"][rows, cols].bitcast(FP8X4),
                        rhs_scale=xq[a]["scales"][rows, cols],
                        start=True,
                        stop=True,
                    )
            for n in range(lo, hi):
                where[a, n] = bank

        def act(eng, a, c, lo, hi):
            src = banks[c][where[a, lo]][:, lo:hi]
            g = 2 * a + c
            col = bias[:, g * QUAD : g * QUAD + 1]
            if eng == "V":
                nc.vector.tensor_scalar(
                    out=relu[a][:, c, lo:hi], in0=src, scalar1=col, scalar2=0.0, op0=ALU.add, op1=ALU.max
                )
            else:
                nc.scalar.activation(out=relu[a][:, c, lo:hi], in_=src, func=ACT.Relu, bias=col)

        def square(eng, a, cs, lo, hi):
            src = relu[a][:, cs[0] : cs[-1] + 1, lo:hi]
            dst = res[a][:, cs[0] : cs[-1] + 1, lo:hi]
            if eng == "V":
                nc.vector.tensor_tensor(out=dst, in0=src, in1=src, op=ALU.mult)
            elif eng == "G":
                nc.gpsimd.tensor_tensor(out=dst, in0=src, in1=src, op=ALU.mult)
            else:
                nc.scalar.activation(out=dst, in_=src, func=ACT.Square)

        def store(a, cs, lo, hi, eng=nc.sync):
            eng.dma_start(
                out=out_pairs[a, :, cs[0] : cs[-1] + 1, lo:hi], in_=res[a][:, cs[0] : cs[-1] + 1, lo:hi]
            )

        def load_bias(eng):
            nc.vector.memset(bias_rows[:], 0.0)
            eng.dma_start(
                out=bias_rows[0:P:QUAD, :].rearrange("q (g i) -> q g i", g=G),
                in_=b.rearrange("g (q i) o -> q g (i o)", i=QUAD),
            )

        def turn_bias():
            nc.vector.transpose(out=bias[:], in_=bias_rows[:])

        with tc.manual_schedule():
            load_x(0, 0, 256)
            load_w(0)
            load_bias(nc.sync)
            load_x(0, 256, 512)
            load_x(1, 0, 256)
            load_w(1)
            load_x(1, 256, 512)
            cast_x("V", 0, 0, 168)
            cast_x("S", 0, 168, 256)
            cast_w("V", 0, 0, 88)
            cast_w("S", 0, 88, 128)
            quant(xq[0], 0, 256)
            quant(wq[0], 0, 128)
            mm(0, 0, 128, 0)
            mm(0, 128, 256, 1, (1, 0))
            turn_bias()
            cast_x("V", 0, 256, 384)
            cast_x("V", 0, 384, 512)
            quant(xq[0], 256, 384)
            mm(0, 256, 384, 2)
            act("S", 0, 0, 0, 128)
            act("S", 0, 1, 0, 128)
            act("S", 0, 0, 128, 256)
            act("V", 0, 1, 128, 256)
            quant(xq[0], 384, 512)
            mm(0, 384, 512, 3, (1, 0))
            square("S", 0, [0, 1], 0, 128)
            square("S", 0, [0, 1], 128, 256)
            store(0, [0], 0, 256)
            store(0, [1], 0, 256)
            cast_x("V", 1, 0, 256)
            cast_w("V", 1)
            act("S", 0, 1, 256, 384)
            act("S", 0, 0, 256, 384)
            act("S", 0, 0, 384, 512)
            act("S", 0, 1, 384, 512)
            quant(xq[1], 0, 128)
            square("V", 0, [1], 256, 320)
            quant(wq[1], 0, 128)
            mm(1, 0, 128, 0, (0, 1))
            quant(xq[1], 128, 256)
            mm(1, 128, 256, 1, (1, 0))
            square("S", 0, [0], 256, 512)
            store(0, [0], 256, 512)
            square("V", 0, [1], 320, 384)
            square("S", 0, [1], 384, 512)
            store(0, [1], 256, 512)
            cast_x("V", 1, 256, 320)
            cast_x("S", 1, 320, 384)
            cast_x("V", 1, 384, 512)
            quant(xq[1], 256, 320)
            quant(xq[1], 320, 384)
            mm(1, 256, 384, 2, (1,))
            quant(xq[1], 384, 512)
            mm(1, 384, 512, 3, (1,))
            mm(1, 256, 384, 2, (0,))
            mm(1, 384, 512, 3, (0,))
            act("S", 1, 1, 0, 128)
            act("S", 1, 1, 128, 256)
            act("S", 1, 0, 0, 128)
            act("S", 1, 0, 128, 256)
            for lo in (0, 128):
                square("V", 1, [1], lo, lo + 128)
            store(1, [1], 0, 256)
            square("S", 1, [0], 0, 128)
            square("S", 1, [0], 128, 256)
            store(1, [0], 0, 256)
            for lo in (256, 384):
                act("S", 1, 0, lo, lo + 128)
                act("V", 1, 1, lo, lo + 128)
            for lo in (256, 384):
                square("S", 1, [0], lo, lo + 128)
                square("V", 1, [1], lo, lo + 128)
            store(1, [1], 256, 512)
            store(1, [0], 256, 512)
